import numpy as np
import ml_dtypes


def mxq(x, axis, fmt="e4m3"):
    dtype, down = {"e4m3": (ml_dtypes.float8_e4m3fn, 7), "e5m2": (ml_dtypes.float8_e5m2, 14)}[fmt]
    v = np.moveaxis(np.asarray(x, np.float32).astype(ml_dtypes.bfloat16).astype(np.float64), axis, -1)
    blocks = v.reshape(v.shape[:-1] + (-1, 32))
    amax = np.abs(blocks).max(-1, keepdims=True)
    byte = np.maximum(np.where(amax > 0, np.frexp(amax)[1] - 1 + 127, 0) - down, 1)
    scale = np.exp2(byte - 127.0)
    codes = (blocks / scale).astype(np.float32).astype(dtype).astype(np.float64)
    return np.moveaxis((codes * scale).reshape(v.shape), -1, axis)


WIDE = False


def mx_kscale(k):
    if not WIDE:
        return np.ones(k)
    levels = np.array([30, -30])
    if k % 512:
        return np.exp2(np.random.permutation(np.resize(levels, k // 32))).repeat(32)
    a = np.empty((k // 512, 16))
    for p in range(k // 512):
        a[p, :8] = np.random.permutation(np.resize(levels, 8))
        for g in range(8):
            far = levels[np.abs(levels - a[p, g]) >= 10]
            a[p, g + 8] = far[np.random.randint(len(far))]
    return np.exp2(a.ravel()).repeat(32)


BF16 = ml_dtypes.bfloat16


def bf(x):
    return np.asarray(x, np.float32).astype(BF16)


def f64(x):
    return np.asarray(x).astype(np.float64)


E2M1 = np.array([0.0, 0.5, 1.0, 1.5, 2.0, 3.0, 4.0, 6.0, -0.0, -0.5, -1.0, -1.5, -2.0, -3.0, -4.0, -6.0])


def pack_weight(w, fmt):
    k, n = w.shape
    w = f64(bf(w)).reshape(k // 32, 32, n)
    amax = np.abs(w).max(1)
    if fmt == "e4m3":
        byte = np.frexp(amax)[1] - 1 + 127 - 7
    else:
        mant, ex = np.frexp(amax / 6.0)
        byte = np.where(mant > 0.5, ex, ex - 1) + 127
    byte = np.clip(np.where(amax > 0, byte, 1), 1, 254)
    scaled = (w * np.exp2(127.0 - byte)[:, None, :]).reshape(k, n).astype(np.float32)
    by_word = np.ascontiguousarray(scaled.reshape(k // 512, 128, 4, n).transpose(0, 1, 3, 2))
    if fmt == "e4m3":
        words = by_word.astype(ml_dtypes.float8_e4m3fn).view(np.uint8)
    else:
        c = by_word.astype(ml_dtypes.float4_e2m1fn).view(np.uint8) & 0xF
        words = c[..., 0::2] | (c[..., 1::2] << 4)
    return np.ascontiguousarray(words), np.ascontiguousarray(byte.astype(np.uint8).reshape(k // 512, 16, n))


def unpack_weight(words, scales, fmt):
    g, p, n, _ = words.shape
    if fmt == "e4m3":
        vals = np.ascontiguousarray(words).view(ml_dtypes.float8_e4m3fn).astype(np.float64)
    else:
        nib = np.empty((g, p, n, 4), np.uint8)
        nib[..., 0::2] = words & 0xF
        nib[..., 1::2] = words >> 4
        vals = E2M1[nib]
    vals = vals * np.repeat(np.exp2(scales.astype(np.float64) - 127.0), 8, axis=1)[..., None]
    return vals.transpose(0, 1, 3, 2).reshape(g * 512, n)
def pack4(w):
    words, scales = pack_weight(w, "e2m1")
    return words.reshape(words.shape[0], 128, -1), scales


def unpack4(words, scales):
    return unpack_weight(words.reshape(words.shape[0], 128, -1, 2), scales, "e2m1")


M, K, N = 1024, 1024, 2048


def setup_inputs():
    s, t = mx_kscale(K), mx_kscale(N)
    a = np.random.standard_normal((K, N)) / np.sqrt(K)
    a_words, a_scales = pack4(a / s[:, None] * t)
    return {"d": bf(np.random.standard_normal((M, K)) * s),
            "a_words": a_words,
            "a_scales": a_scales,
            "c": bf(0.5 * np.random.standard_normal((M, N)) * t),
            "w": bf(np.exp(0.5 * np.random.standard_normal(N))),
            "b": bf(a.T / t[:, None]),
            "prior": bf(0.5 * np.random.standard_normal((M, K)))}


def reference(d, a_words, a_scales, c, w, b, prior):
    v = mxq(f64(d), 1, "e4m3") @ unpack4(a_words, a_scales)
    r = (v - f64(c)) * f64(w)
    grad = mxq(r, 1, "e5m2") @ mxq(f64(b), 0, "e4m3")
    return grad + f64(prior)

@@ -1,0 +1,317 @@
+from contextlib import ExitStack
+
+import concourse.mybir as mybir
+from concourse.masks import make_identity
+
+M, K, N = 1024, 1024, 2048
+FLOPS = 2 * 2 * M * K * N
+
+F32 = mybir.dt.float32
+BF16 = mybir.dt.bfloat16
+I32 = mybir.dt.int32
+U32 = mybir.dt.uint32
+U8 = mybir.dt.uint8
+E4M3 = mybir.dt.float8_e4m3fn_x4
+E5M2 = mybir.dt.float8_e5m2_x4
+E2M1 = mybir.dt.float4_e2m1fn_x4
+ALU = mybir.AluOpType
+
+P = 128
+BANK = 512
+ROW_TILES = M // P
+K_PASSES = K // 512
+N_GROUPS = N // 512
+K_HALVES = K // BANK
+GP_GROUPS = 2
+OUT_BUFS = 6
+
+
+def tile_demand_estimation_gradient_s9_kernel(tc, d, a_words, a_scales, c, w, b, prior, out):
+    nc = tc.nc
+    with ExitStack() as ctx:
+        sb = ctx.enter_context(tc.tile_pool(name="sb", bufs=1))
+        ps = ctx.enter_context(tc.psum_pool(name="ps", bufs=1))
+        ctx.enter_context(tc.manual_schedule())
+
+        def sbuf(name, shape, dtype):
+            return sb.tile(shape, dtype, name=name, align_bytes=64)
+
+        ident = sbuf("ident", [P, P], F32)
+        d_raw = [sbuf("d_raw%d" % i, [P, K], BF16) for i in range(ROW_TILES)]
+        d_t = [sbuf("d_t%d" % s, [P, K], BF16) for s in range(2)]
+        d_codes = [sbuf("d_codes%d" % i, [P, K // 4], U32) for i in range(ROW_TILES)]
+        d_scales = [sbuf("d_scales%d" % i, [P, K // 4], U8) for i in range(ROW_TILES)]
+        a_codes = [sbuf("a_codes%d" % g, [P, K_PASSES, 2 * BANK], U8) for g in range(N_GROUPS)]
+        a_plane = sbuf("a_plane", [P, K_PASSES, N], U8)
+        c_raw = [[sbuf("c_raw%d_%d" % (i, h), [P, N // 2], BF16) for h in range(2)] for i in range(ROW_TILES)]
+        w_rows = sbuf("w_rows", [P, N // P], BF16)
+        w_all = sbuf("w_all", [P, N], BF16)
+        b_raw = [[sbuf("b_raw%d_%d" % (g, h), [P, 4, BANK], BF16) for h in range(K_HALVES)] for g in range(N_GROUPS)]
+        b_grp = [sbuf("b_grp%d" % s, [P, 4 * BANK], BF16) for s in range(4)]
+        b_codes = [[sbuf("b_codes%d_%d" % (g, h), [P, BANK], U32) for h in range(K_HALVES)] for g in range(N_GROUPS)]
+        b_scales = [[sbuf("b_scales%d_%d" % (g, h), [P, BANK], U8) for h in range(K_HALVES)] for g in range(N_GROUPS)]
+        prior_sb = [sbuf("prior%d" % i, [P, K], BF16) for i in range(ROW_TILES)]
+        diff = [sbuf("diff%d" % s, [P, N], F32) for s in range(2)]
+        resid = [sbuf("resid%d" % s, [P, N], BF16) for s in range(2)]
+        resid_t = [sbuf("resid_t%d" % s, [P, N], BF16) for s in range(2)]
+        r_codes = [sbuf("r_codes%d" % i, [P, N // 4], U32) for i in range(ROW_TILES)]
+        r_scales = [sbuf("r_scales%d" % i, [P, N // 4], U8) for i in range(ROW_TILES)]
+        result = [sbuf("result%d" % s, [P, BANK], F32) for s in range(OUT_BUFS)]
+
+        v_bank = [ps.tile([P, BANK], F32, name="v_bank%d" % g) for g in range(N_GROUPS)]
+        o_bank = [ps.tile([P, BANK], F32, name="o_bank%d" % s) for s in range(2)]
+        t_bank = [ps.tile([P, BANK], F32, name="t_bank%d" % s) for s in range(2)]
+
+        def rows(i):
+            return slice(i * P, (i + 1) * P)
+
+        def cols(g):
+            return slice(g * BANK, (g + 1) * BANK)
+
+        def load_d(i):
+            nc.sync.dma_start(out=d_raw[i][:], in_=d[rows(i), :])
+
+        def load_c(i, h):
+            nc.sync.dma_start(out=c_raw[i][h][:], in_=c[rows(i), h * (N // 2) : (h + 1) * (N // 2)])
+
+        def load_a(g):
+            src = a_words[:, :, 2 * BANK * g : 2 * BANK * (g + 1)].rearrange("s p x -> p s x")
+            nc.sync.dma_start(out=a_codes[g][:].bitcast(I32), in_=src.bitcast(I32))
+
+        def load_a_scales():
+            nc.vector.memset(a_plane[:].rearrange("p s n -> p (s n)").bitcast(I32), 0)
+            for q in range(4):
+                src = a_scales[:, 4 * q : 4 * q + 4, :].rearrange("s r n -> r s n")
+                nc.sync.dma_start(out=a_plane[32 * q : 32 * q + 4, :, :].bitcast(I32), in_=src.bitcast(I32))
+
+        def load_b(g, h):
+            src = b[cols(g), cols(h)].rearrange("(p t) k -> p t k", t=4)
+            nc.sync.dma_start(out=b_raw[g][h][:], in_=src)
+
+        def load_prior(i):
+            nc.sync.dma_start(out=prior_sb[i][:], in_=prior[rows(i), :])
+
+        def turn_d(i, bank):
+            words = d_raw[i][:].bitcast(F32)
+            for s in range(K_PASSES):
+                for u in range(2):
+                    at = (2 * s + u) * P
+                    nc.tensor.transpose(bank[:, at : at + P], words[:, 256 * s + u : 256 * (s + 1) : 2], ident[:])
+
+        def pair_up(copy, dst, bank, groups):
+            width = groups * 2 * P
+            copy(
+                out=dst.bitcast(F32).rearrange("p (g m u) -> p g m u", g=groups, u=2),
+                in_=bank[:, 0:width].rearrange("p (g u m) -> p g m u", g=groups, u=2),
+            )
+
+        def quantize_d(i):
+            nc.vector.quantize_mx(out=d_codes[i][:].bitcast(E4M3), scales=d_scales[i][:], in_=d_t[i % 2][:])
+
+        def spread_w():
+            words = w_rows[:].bitcast(F32)
+            for u in range(2):
+                for j in range(4):
+                    col = 2 * j + u
+                    nc.tensor.transpose(
+                        t_bank[u][:, j * P : (j + 1) * P], words[:, col : col + 1].to_broadcast([P, P]), ident[:]
+                    )
+                dst = w_all[:].bitcast(F32).rearrange("p (g u a j) -> p u g a j", g=N_GROUPS, u=2, j=4)
+                nc.scalar.copy(
+                    out=dst[:, u], in_=t_bank[u][:].rearrange("p (j g a) -> p g a j", j=4, g=N_GROUPS)
+                )
+
+        def first_product(i, g):
+            for s in range(K_PASSES):
+                nc.tensor.matmul_mx(
+                    out=v_bank[g][:],
+                    lhsT=d_codes[i][:, s * P : (s + 1) * P].bitcast(E4M3),
+                    lhsT_scale=d_scales[i][:, s * P : (s + 1) * P],
+                    rhs=a_codes[g][:, s, :].bitcast(E2M1),
+                    rhs_scale=a_plane[:, s, cols(g)],
+                    start=(s == 0),
+                    stop=(s == K_PASSES - 1),
+                )
+
+        def subtract(i, g):
+            order = "p (j u e) -> p u j e"
+            counts = c_raw[i][g // 2][:, cols(g % 2)]
+            nc.vector.tensor_tensor(
+                out=diff[i % 2][:, cols(g)].rearrange("p (u j e) -> p u j e", u=2, e=2),
+                in0=v_bank[g][:].rearrange(order, u=2, e=2),
+                in1=counts.rearrange(order, u=2, e=2),
+                op=ALU.subtract,
+            )
+
+        def weigh(engine, i, g0, g1):
+            span = slice(g0 * BANK, g1 * BANK)
+            engine.tensor_tensor(out=resid[i % 2][:, span], in0=diff[i % 2][:, span], in1=w_all[:, span], op=ALU.mult)
+
+        def turn_r(i, g0, g1):
+            bank = t_bank[g0 // 2]
+            words = resid[i % 2][:].bitcast(F32)
+            at = (g0 % 2) * 2 * P
+            for x in range(2 * (g1 - g0)):
+                first = 2 * g0 * P + x * P
+                nc.tensor.transpose(bank[:, at + x * P : at + (x + 1) * P], words[:, first : first + P], ident[:])
+            pair_up(nc.scalar.copy, resid_t[i % 2][:, g0 * BANK : g1 * BANK], bank[:, at:BANK], g1 - g0)
+
+        def quantize_r(i, g0, g1):
+            nc.vector.quantize_mx(
+                out=r_codes[i][:, g0 * P : g1 * P].bitcast(E5M2),
+                scales=r_scales[i][:, g0 * P : g1 * P],
+                in_=resid_t[i % 2][:, g0 * BANK : g1 * BANK],
+            )
+
+        b_order = [(g, h) for h in range(K_HALVES) for g in range(N_GROUPS)]
+
+        def group_b(x):
+            g, h = b_order[x]
+            nc.scalar.copy(
+                out=b_grp[x % 4][:].rearrange("p (a i t) -> p a t i", i=4, t=4),
+                in_=b_raw[g][h][:].rearrange("p t (a i) -> p a t i", i=4),
+            )
+
+        def quantize_b(x):
+            g, h = b_order[x]
+            nc.vector.quantize_mx(out=b_codes[g][h][:].bitcast(E4M3), scales=b_scales[g][h][:], in_=b_grp[x % 4][:])
+
+        def second_product(i, h, bank, g0, g1):
+            for g in range(g0, g1):
+                nc.tensor.matmul_mx(
+                    out=bank[:],
+                    lhsT=r_codes[i][:, g * P : (g + 1) * P].bitcast(E5M2),
+                    lhsT_scale=r_scales[i][:, g * P : (g + 1) * P],
+                    rhs=b_codes[g][h][:].bitcast(E4M3),
+                    rhs_scale=b_scales[g][h][:],
+                    start=(g == 0),
+                    stop=(g == N_GROUPS - 1),
+                )
+
+        def finish(x, i, h):
+            stage = result[x % OUT_BUFS]
+            nc.vector.tensor_tensor(out=stage[:], in0=o_bank[x % 2][:], in1=prior_sb[i][:, cols(h)], op=ALU.add)
+            nc.sync.dma_start(out=out[rows(i), cols(h)], in_=stage[:])
+
+        make_identity(nc, ident[:])
+        load_d(0)
+        load_a_scales()
+        nc.sync.dma_start(out=w_rows[:], in_=w.rearrange("(p x) -> p x", p=P))
+        load_a(0)
+        load_d(1)
+        load_c(0, 0)
+        load_a(1)
+        load_a(2)
+        load_a(3)
+        load_c(0, 1)
+        load_b(*b_order[0])
+        load_d(2)
+        load_d(3)
+        load_b(*b_order[1])
+        for i in range(1, ROW_TILES):
+            load_c(i, 0)
+            load_c(i, 1)
+            for x in range(2 * i, min(2 * i + 2, len(b_order))):
+                load_b(*b_order[x])
+            if i == 1:
+                load_d(4)
+                load_d(5)
+            if i == 2:
+                load_d(6)
+                load_d(7)
+            if i >= 2:
+                load_prior(i - 2)
+        load_prior(ROW_TILES - 2)
+        load_prior(ROW_TILES - 1)
+
+        turn_d(0, o_bank[0])
+        pair_up(nc.vector.tensor_copy, d_t[0][:], o_bank[0], K_PASSES)
+        quantize_d(0)
+        spread_w()
+        first_product(0, 0)
+        turn_d(1, o_bank[1])
+        pair_up(nc.vector.tensor_copy, d_t[1][:], o_bank[1], K_PASSES)
+        first_product(0, 1)
+        quantize_d(1)
+        first_product(0, 2)
+        first_product(0, 3)
+
+        last = ROW_TILES - 1
+        plan = {
+            2: ([], [(0, 0)]),
+            3: ([], [(1, 0)]),
+            4: ([], [(2, 0), (0, 1)]),
+            5: ([(3, 0)], [(1, 1), (4, 0)]),
+            6: ([(2, 1)], [(3, 1), (5, 0)]),
+            7: ([(4, 1)], [(5, 1)]),
+        }
+        turn_plan = {0: [2, 3], 1: [4, 5], 2: [6, 7]}
+        pending = []
+        issued = []
+
+        def multiply(blocks):
+            for i, h in blocks:
+                x = len(issued)
+                issued.append((i, h))
+                second_product(i, h, o_bank[x % 2], 0, N_GROUPS)
+                pending.append((x, i, h))
+
+        def drain(count):
+            for y in range(min(count, len(pending))):
+                finish(*pending[0])
+                pending.remove(pending[0])
+
+        for i in range(ROW_TILES):
+            early, late = plan.get(i, ([], []))
+            grouping = i < N_GROUPS
+            turned = turn_plan.get(i, [])
+            if early:
+                drain(1)
+            for t in turned:
+                turn_d(t, o_bank[t % 2])
+            if not grouping:
+                turn_r(i - 1, 0, 2)
+                turn_r(i - 1, 2, 4)
+            multiply(early)
+            if grouping:
+                group_b(2 * i)
+                group_b(2 * i + 1)
+            for g in range(N_GROUPS):
+                subtract(i, g)
+                if g < GP_GROUPS:
+                    weigh(nc.gpsimd, i, g, g + 1)
+            if i < last:
+                for g in range(N_GROUPS):
+                    first_product(i + 1, g)
+            if i > 0 and grouping:
+                turn_r(i - 1, 0, 2)
+                turn_r(i - 1, 2, 4)
+            drain(2)
+            for t in turned:
+                pair_up(nc.vector.tensor_copy, d_t[t % 2][:], o_bank[t % 2], K_PASSES)
+            if 2 <= i <= N_GROUPS:
+                quantize_r(i - 2, 0, N_GROUPS)
+            if 0 < i <= N_GROUPS:
+                quantize_b(2 * i - 2)
+                quantize_b(2 * i - 1)
+            if not grouping:
+                quantize_r(i - 1, 0, N_GROUPS)
+            if i < last:
+                weigh(nc.vector, i, GP_GROUPS, N_GROUPS)
+            for t in turned:
+                quantize_d(t)
+            multiply(late)
+
+        turn_r(last, 0, 2)
+        multiply([(last - 1, 0)])
+        weigh(nc.vector, last, 2, 3)
+        drain(1)
+        weigh(nc.vector, last, 3, 4)
+        quantize_r(last, 0, 2)
+        turn_r(last, 2, 4)
+        multiply([(last - 1, 1)])
+        drain(1)
+        quantize_r(last, 2, 4)
+        drain(1)
+        multiply([(last, 0), (last, 1)])
+        drain(2)

@@ -24,6 +24,7 @@ N_GROUPS = N // 512
 K_HALVES = K // BANK
 GP_GROUPS = 2
 OUT_BUFS = 6
+B_SHIFT = 0
 
 
 def tile_demand_estimation_gradient_s9_kernel(tc, d, a_words, a_scales, c, w, b, prior, out):
@@ -38,18 +39,18 @@ def tile_demand_estimation_gradient_s9_kernel(tc, d, a_words, a_scales, c, w, b,
 
         ident = sbuf("ident", [P, P], F32)
         d_raw = [sbuf("d_raw%d" % i, [P, K], BF16) for i in range(ROW_TILES)]
-        d_t = [sbuf("d_t%d" % s, [P, K], BF16) for s in range(2)]
-        d_codes = [sbuf("d_codes%d" % i, [P, K // 4], U32) for i in range(ROW_TILES)]
-        d_scales = [sbuf("d_scales%d" % i, [P, K // 4], U8) for i in range(ROW_TILES)]
+        d_t = sbuf("d_t", [P, 4 * K], BF16)
+        d_codes = sbuf("d_codes", [P, ROW_TILES * K // 4], U32)
+        d_scales = sbuf("d_scales", [P, ROW_TILES * K // 4], U8)
         a_codes = [sbuf("a_codes%d" % g, [P, K_PASSES, 2 * BANK], U8) for g in range(N_GROUPS)]
         a_plane = sbuf("a_plane", [P, K_PASSES, N], U8)
         c_raw = [[sbuf("c_raw%d_%d" % (i, h), [P, N // 2], BF16) for h in range(2)] for i in range(ROW_TILES)]
         w_rows = sbuf("w_rows", [P, N // P], BF16)
         w_all = sbuf("w_all", [P, N], BF16)
         b_raw = [[sbuf("b_raw%d_%d" % (g, h), [P, 4, BANK], BF16) for h in range(K_HALVES)] for g in range(N_GROUPS)]
-        b_grp = [sbuf("b_grp%d" % s, [P, 4 * BANK], BF16) for s in range(4)]
-        b_codes = [[sbuf("b_codes%d_%d" % (g, h), [P, BANK], U32) for h in range(K_HALVES)] for g in range(N_GROUPS)]
-        b_scales = [[sbuf("b_scales%d_%d" % (g, h), [P, BANK], U8) for h in range(K_HALVES)] for g in range(N_GROUPS)]
+        b_grp = sbuf("b_grp", [P, 4 * 4 * BANK], BF16)
+        b_codes = sbuf("b_codes", [P, K_HALVES * N_GROUPS * BANK], U32)
+        b_scales = sbuf("b_scales", [P, K_HALVES * N_GROUPS * BANK], U8)
         prior_sb = [sbuf("prior%d" % i, [P, K], BF16) for i in range(ROW_TILES)]
         diff = [sbuf("diff%d" % s, [P, N], F32) for s in range(2)]
         resid = [sbuf("resid%d" % s, [P, N], BF16) for s in range(2)]
@@ -105,8 +106,13 @@ def tile_demand_estimation_gradient_s9_kernel(tc, d, a_words, a_scales, c, w, b,
                 in_=bank[:, 0:width].rearrange("p (g u m) -> p g m u", g=groups, u=2),
             )
 
-        def quantize_d(i):
-            nc.vector.quantize_mx(out=d_codes[i][:].bitcast(E4M3), scales=d_scales[i][:], in_=d_t[i % 2][:])
+        def d_stage(i, count=1):
+            slot = i % 4
+            return d_t[:, slot * K : (slot + count) * K]
+
+        def quantize_d(i, count=1):
+            span = slice(i * K // 4, (i + count) * K // 4)
+            nc.vector.quantize_mx(out=d_codes[:, span].bitcast(E4M3), scales=d_scales[:, span], in_=d_stage(i, count))
 
         def spread_w():
             words = w_rows[:].bitcast(F32)
@@ -125,8 +131,8 @@ def tile_demand_estimation_gradient_s9_kernel(tc, d, a_words, a_scales, c, w, b,
             for s in range(K_PASSES):
                 nc.tensor.matmul_mx(
                     out=v_bank[g][:],
-                    lhsT=d_codes[i][:, s * P : (s + 1) * P].bitcast(E4M3),
-                    lhsT_scale=d_scales[i][:, s * P : (s + 1) * P],
+                    lhsT=d_codes[:, (2 * i + s) * P : (2 * i + s + 1) * P].bitcast(E4M3),
+                    lhsT_scale=d_scales[:, (2 * i + s) * P : (2 * i + s + 1) * P],
                     rhs=a_codes[g][:, s, :].bitcast(E2M1),
                     rhs_scale=a_plane[:, s, cols(g)],
                     start=(s == 0),
@@ -134,17 +140,16 @@ def tile_demand_estimation_gradient_s9_kernel(tc, d, a_words, a_scales, c, w, b,
                 )
 
         def subtract(i, g):
-            order = "p (j u e) -> p u j e"
-            counts = c_raw[i][g // 2][:, cols(g % 2)]
+            natural = "p (j u e) -> p j u e"
             nc.vector.tensor_tensor(
-                out=diff[i % 2][:, cols(g)].rearrange("p (u j e) -> p u j e", u=2, e=2),
-                in0=v_bank[g][:].rearrange(order, u=2, e=2),
-                in1=counts.rearrange(order, u=2, e=2),
+                out=diff[i % 2][:, cols(g)].rearrange("p (u j e) -> p j u e", u=2, e=2),
+                in0=v_bank[g][:].rearrange(natural, u=2, e=2),
+                in1=c_raw[i][g // 2][:, cols(g % 2)].rearrange(natural, u=2, e=2),
                 op=ALU.subtract,
             )
 
-        def weigh(engine, i, g0, g1):
-            span = slice(g0 * BANK, g1 * BANK)
+        def weigh(engine, i, c0, c1):
+            span = slice(c0, c1)
             engine.tensor_tensor(out=resid[i % 2][:, span], in0=diff[i % 2][:, span], in1=w_all[:, span], op=ALU.mult)
 
         def turn_r(i, g0, g1):
@@ -165,16 +170,20 @@ def tile_demand_estimation_gradient_s9_kernel(tc, d, a_words, a_scales, c, w, b,
 
         b_order = [(g, h) for h in range(K_HALVES) for g in range(N_GROUPS)]
 
-        def group_b(x):
+        def b_stage(x, count=1):
+            slot = (x + B_SHIFT) % 4
+            return b_grp[:, slot * 4 * BANK : (slot + count) * 4 * BANK]
+
+        def group_b(x, copy):
             g, h = b_order[x]
-            nc.scalar.copy(
-                out=b_grp[x % 4][:].rearrange("p (a i t) -> p a t i", i=4, t=4),
+            copy(
+                out=b_stage(x).rearrange("p (a i t) -> p a t i", i=4, t=4),
                 in_=b_raw[g][h][:].rearrange("p t (a i) -> p a t i", i=4),
             )
 
-        def quantize_b(x):
-            g, h = b_order[x]
-            nc.vector.quantize_mx(out=b_codes[g][h][:].bitcast(E4M3), scales=b_scales[g][h][:], in_=b_grp[x % 4][:])
+        def quantize_b(x, count=1):
+            span = slice(x * BANK, (x + count) * BANK)
+            nc.vector.quantize_mx(out=b_codes[:, span].bitcast(E4M3), scales=b_scales[:, span], in_=b_stage(x, count))
 
         def second_product(i, h, bank, g0, g1):
             for g in range(g0, g1):
@@ -182,136 +191,131 @@ def tile_demand_estimation_gradient_s9_kernel(tc, d, a_words, a_scales, c, w, b,
                     out=bank[:],
                     lhsT=r_codes[i][:, g * P : (g + 1) * P].bitcast(E5M2),
                     lhsT_scale=r_scales[i][:, g * P : (g + 1) * P],
-                    rhs=b_codes[g][h][:].bitcast(E4M3),
-                    rhs_scale=b_scales[g][h][:],
+                    rhs=b_codes[:, cols(h * N_GROUPS + g)].bitcast(E4M3),
+                    rhs_scale=b_scales[:, cols(h * N_GROUPS + g)],
                     start=(g == 0),
                     stop=(g == N_GROUPS - 1),
                 )
 
-        def finish(x, i, h):
+        def finish(x, i, h, bank):
             stage = result[x % OUT_BUFS]
-            nc.vector.tensor_tensor(out=stage[:], in0=o_bank[x % 2][:], in1=prior_sb[i][:, cols(h)], op=ALU.add)
+            nc.vector.tensor_tensor(out=stage[:], in0=bank[:], in1=prior_sb[i][:, cols(h)], op=ALU.add)
             nc.sync.dma_start(out=out[rows(i), cols(h)], in_=stage[:])
 
         make_identity(nc, ident[:])
+        last = ROW_TILES - 1
+        nc.sync.dma_start(out=w_rows[:], in_=w.rearrange("(p x) -> p x", p=P))
         load_d(0)
         load_a_scales()
-        nc.sync.dma_start(out=w_rows[:], in_=w.rearrange("(p x) -> p x", p=P))
         load_a(0)
-        load_d(1)
         load_c(0, 0)
+        load_d(1)
         load_a(1)
         load_a(2)
-        load_a(3)
         load_c(0, 1)
         load_b(*b_order[0])
-        load_d(2)
-        load_d(3)
-        load_b(*b_order[1])
-        for i in range(1, ROW_TILES):
-            load_c(i, 0)
-            load_c(i, 1)
-            for x in range(2 * i, min(2 * i + 2, len(b_order))):
+        load_a(3)
+        for i in range(last):
+            if i % 2 == 0 and i + 3 <= last:
+                load_d(i + 2)
+                load_d(i + 3)
+            for x in range(max(1, 2 * i), min(2 * i + 2, len(b_order))):
                 load_b(*b_order[x])
-            if i == 1:
-                load_d(4)
-                load_d(5)
+            load_c(i + 1, 0)
+            load_c(i + 1, 1)
             if i == 2:
-                load_d(6)
-                load_d(7)
+                load_prior(0)
             if i >= 2:
-                load_prior(i - 2)
-        load_prior(ROW_TILES - 2)
-        load_prior(ROW_TILES - 1)
+                load_prior(i - 1)
+        load_prior(last - 1)
+        load_prior(last)
 
         turn_d(0, o_bank[0])
-        pair_up(nc.vector.tensor_copy, d_t[0][:], o_bank[0], K_PASSES)
+        pair_up(nc.vector.tensor_copy, d_stage(0), o_bank[0], K_PASSES)
         quantize_d(0)
         spread_w()
         first_product(0, 0)
         turn_d(1, o_bank[1])
-        pair_up(nc.vector.tensor_copy, d_t[1][:], o_bank[1], K_PASSES)
-        first_product(0, 1)
-        quantize_d(1)
-        first_product(0, 2)
-        first_product(0, 3)
+        pair_up(nc.scalar.copy, d_stage(1), o_bank[1], K_PASSES)
+        for g in range(1, N_GROUPS):
+            first_product(0, g)
 
-        last = ROW_TILES - 1
-        plan = {
-            2: ([], [(0, 0)]),
-            3: ([], [(1, 0)]),
-            4: ([], [(2, 0), (0, 1)]),
-            5: ([(3, 0)], [(1, 1), (4, 0)]),
-            6: ([(2, 1)], [(3, 1), (5, 0)]),
-            7: ([(4, 1)], [(5, 1)]),
-        }
-        turn_plan = {0: [2, 3], 1: [4, 5], 2: [6, 7]}
+        todo = [(i, h) for i in range(ROW_TILES) for h in range(K_HALVES)]
         pending = []
         issued = []
 
-        def multiply(blocks):
-            for i, h in blocks:
-                x = len(issued)
+        def multiply(count, tiles_ready, halves_ready, banks):
+            ready = [(i, h) for i, h in todo if i < tiles_ready and h < halves_ready]
+            for i, h in ready[:count]:
+                bank = banks[len(issued) % len(banks)]
+                second_product(i, h, bank, 0, N_GROUPS)
+                pending.append((len(issued), i, h, bank))
                 issued.append((i, h))
-                second_product(i, h, o_bank[x % 2], 0, N_GROUPS)
-                pending.append((x, i, h))
+                todo.remove((i, h))
 
         def drain(count):
-            for y in range(min(count, len(pending))):
-                finish(*pending[0])
-                pending.remove(pending[0])
+            for block in pending[:count]:
+                finish(*block)
+                pending.remove(block)
+
+        def turn_d_pair(t, banks):
+            for y in range(2):
+                turn_d(t + y, banks[y])
+                pair_up(nc.scalar.copy, d_stage(t + y), banks[y], K_PASSES)
 
         for i in range(ROW_TILES):
-            early, late = plan.get(i, ([], []))
-            grouping = i < N_GROUPS
-            turned = turn_plan.get(i, [])
-            if early:
+            halves_before = max(0, (i - 1) // 2)
+            halves_after = i // 2
+            turning = i % 2 == 0 and i + 3 <= last
+            if len(pending) == 2 and halves_before >= K_HALVES:
                 drain(1)
-            for t in turned:
-                turn_d(t, o_bank[t % 2])
-            if not grouping:
+            if i == 0:
+                group_b(0, nc.scalar.copy)
+            else:
                 turn_r(i - 1, 0, 2)
                 turn_r(i - 1, 2, 4)
-            multiply(early)
-            if grouping:
-                group_b(2 * i)
-                group_b(2 * i + 1)
+            turn_late = len(pending) > 0
+            if turning and not turn_late:
+                turn_d_pair(i + 2, o_bank)
+            finishing = len(pending)
+            if halves_before >= K_HALVES:
+                multiply(1, i - 1, halves_before, o_bank)
+            finishing = len(pending)
+            for x in range(max(1, 2 * i), min(2 * i + 2, len(b_order))):
+                group_b(x, nc.scalar.copy)
+            share = BANK if i == last else BANK + finishing * BANK // 2
             for g in range(N_GROUPS):
                 subtract(i, g)
-                if g < GP_GROUPS:
-                    weigh(nc.gpsimd, i, g, g + 1)
-            if i < last:
-                for g in range(N_GROUPS):
-                    first_product(i + 1, g)
-            if i > 0 and grouping:
-                turn_r(i - 1, 0, 2)
-                turn_r(i - 1, 2, 4)
+                if g == 0:
+                    weigh(nc.gpsimd, i, 0, BANK)
+                if g == 1 and share > BANK:
+                    weigh(nc.gpsimd, i, BANK, share)
+            if i == last:
+                break
+            if i == 0:
+                quantize_d(1)
+            for g in range(N_GROUPS):
+                first_product(i + 1, g)
+            if turning and turn_late:
+                turn_d_pair(i + 2, [o_bank[len(issued) % 2], t_bank[0]])
             drain(2)
-            for t in turned:
-                pair_up(nc.vector.tensor_copy, d_t[t % 2][:], o_bank[t % 2], K_PASSES)
-            if 2 <= i <= N_GROUPS:
-                quantize_r(i - 2, 0, N_GROUPS)
             if 0 < i <= N_GROUPS:
-                quantize_b(2 * i - 2)
-                quantize_b(2 * i - 1)
-            if not grouping:
+                quantize_b(2 * i - 2, 2)
+            if i > 0:
                 quantize_r(i - 1, 0, N_GROUPS)
-            if i < last:
-                weigh(nc.vector, i, GP_GROUPS, N_GROUPS)
-            for t in turned:
-                quantize_d(t)
-            multiply(late)
+            weigh(nc.vector, i, share, N)
+            if turning:
+                quantize_d(i + 2, 2)
+            multiply(2, i, halves_after, o_bank)
 
+        quantize_r(last - 1, 0, N_GROUPS)
+        weigh(nc.vector, last, BANK, N)
+        multiply(1, last, K_HALVES, v_bank)
         turn_r(last, 0, 2)
-        multiply([(last - 1, 0)])
-        weigh(nc.vector, last, 2, 3)
-        drain(1)
-        weigh(nc.vector, last, 3, 4)
-        quantize_r(last, 0, 2)
         turn_r(last, 2, 4)
-        multiply([(last - 1, 1)])
-        drain(1)
-        quantize_r(last, 2, 4)
-        drain(1)
-        multiply([(last, 0), (last, 1)])
         drain(2)
+        multiply(1, last, K_HALVES, v_bank)
+        quantize_r(last, 0, 2)
+        quantize_r(last, 2, 4)
+        multiply(2, ROW_TILES, K_HALVES, v_bank)
+        drain(4)

@@ -17,14 +17,18 @@ E2M1 = mybir.dt.float4_e2m1fn_x4
 ALU = mybir.AluOpType
 
 P = 128
+PACK = 4
+PASS = P * PACK
 BANK = 512
 ROW_TILES = M // P
-K_PASSES = K // 512
-N_GROUPS = N // 512
+LAST = ROW_TILES - 1
+K_PASSES = K // PASS
+N_GROUPS = N // PASS
 K_HALVES = K // BANK
-GP_GROUPS = 2
-OUT_BUFS = 6
-B_SHIFT = 0
+B_PIECES = K_HALVES * N_GROUPS
+RING = 4
+RESULT_BUFS = 6
+GPSIMD_COLUMNS_PER_BLOCK = BANK // 2
 
 
 def tile_demand_estimation_gradient_s9_kernel(tc, d, a_words, a_scales, c, w, b, prior, out):
@@ -39,29 +43,29 @@ def tile_demand_estimation_gradient_s9_kernel(tc, d, a_words, a_scales, c, w, b,
 
         ident = sbuf("ident", [P, P], F32)
         d_raw = [sbuf("d_raw%d" % i, [P, K], BF16) for i in range(ROW_TILES)]
-        d_t = sbuf("d_t", [P, 4 * K], BF16)
-        d_codes = sbuf("d_codes", [P, ROW_TILES * K // 4], U32)
-        d_scales = sbuf("d_scales", [P, ROW_TILES * K // 4], U8)
+        d_turned = sbuf("d_turned", [P, RING * K], BF16)
+        d_codes = sbuf("d_codes", [P, ROW_TILES * K // PACK], U32)
+        d_scales = sbuf("d_scales", [P, ROW_TILES * K // PACK], U8)
         a_codes = [sbuf("a_codes%d" % g, [P, K_PASSES, 2 * BANK], U8) for g in range(N_GROUPS)]
-        a_plane = sbuf("a_plane", [P, K_PASSES, N], U8)
-        c_raw = [[sbuf("c_raw%d_%d" % (i, h), [P, N // 2], BF16) for h in range(2)] for i in range(ROW_TILES)]
+        a_scale_sb = sbuf("a_scale_sb", [P, K_PASSES, N], U8)
+        c_raw = [[sbuf("c_raw%d_%d" % (i, y), [P, N // 2], BF16) for y in range(2)] for i in range(ROW_TILES)]
         w_rows = sbuf("w_rows", [P, N // P], BF16)
         w_all = sbuf("w_all", [P, N], BF16)
-        b_raw = [[sbuf("b_raw%d_%d" % (g, h), [P, 4, BANK], BF16) for h in range(K_HALVES)] for g in range(N_GROUPS)]
-        b_grp = sbuf("b_grp", [P, 4 * 4 * BANK], BF16)
-        b_codes = sbuf("b_codes", [P, K_HALVES * N_GROUPS * BANK], U32)
-        b_scales = sbuf("b_scales", [P, K_HALVES * N_GROUPS * BANK], U8)
+        b_raw = [[sbuf("b_raw%d_%d" % (g, h), [P, PACK, BANK], BF16) for h in range(K_HALVES)] for g in range(N_GROUPS)]
+        b_grouped = sbuf("b_grouped", [P, RING * PACK * BANK], BF16)
+        b_codes = sbuf("b_codes", [P, B_PIECES * BANK], U32)
+        b_scales = sbuf("b_scales", [P, B_PIECES * BANK], U8)
         prior_sb = [sbuf("prior%d" % i, [P, K], BF16) for i in range(ROW_TILES)]
-        diff = [sbuf("diff%d" % s, [P, N], F32) for s in range(2)]
-        resid = [sbuf("resid%d" % s, [P, N], BF16) for s in range(2)]
-        resid_t = [sbuf("resid_t%d" % s, [P, N], BF16) for s in range(2)]
-        r_codes = [sbuf("r_codes%d" % i, [P, N // 4], U32) for i in range(ROW_TILES)]
-        r_scales = [sbuf("r_scales%d" % i, [P, N // 4], U8) for i in range(ROW_TILES)]
-        result = [sbuf("result%d" % s, [P, BANK], F32) for s in range(OUT_BUFS)]
+        diff = [sbuf("diff%d" % y, [P, N], F32) for y in range(2)]
+        resid = [sbuf("resid%d" % y, [P, N], BF16) for y in range(2)]
+        resid_turned = [sbuf("resid_turned%d" % y, [P, N], BF16) for y in range(2)]
+        r_codes = [sbuf("r_codes%d" % i, [P, N // PACK], U32) for i in range(ROW_TILES)]
+        r_scales = [sbuf("r_scales%d" % i, [P, N // PACK], U8) for i in range(ROW_TILES)]
+        result = [sbuf("result%d" % y, [P, BANK], F32) for y in range(RESULT_BUFS)]
 
         v_bank = [ps.tile([P, BANK], F32, name="v_bank%d" % g) for g in range(N_GROUPS)]
-        o_bank = [ps.tile([P, BANK], F32, name="o_bank%d" % s) for s in range(2)]
-        t_bank = [ps.tile([P, BANK], F32, name="t_bank%d" % s) for s in range(2)]
+        o_bank = [ps.tile([P, BANK], F32, name="o_bank%d" % y) for y in range(2)]
+        t_bank = [ps.tile([P, BANK], F32, name="t_bank%d" % y) for y in range(2)]
 
         def rows(i):
             return slice(i * P, (i + 1) * P)
@@ -72,22 +76,22 @@ def tile_demand_estimation_gradient_s9_kernel(tc, d, a_words, a_scales, c, w, b,
         def load_d(i):
             nc.sync.dma_start(out=d_raw[i][:], in_=d[rows(i), :])
 
-        def load_c(i, h):
-            nc.sync.dma_start(out=c_raw[i][h][:], in_=c[rows(i), h * (N // 2) : (h + 1) * (N // 2)])
+        def load_c(i, y):
+            nc.sync.dma_start(out=c_raw[i][y][:], in_=c[rows(i), y * (N // 2) : (y + 1) * (N // 2)])
 
         def load_a(g):
             src = a_words[:, :, 2 * BANK * g : 2 * BANK * (g + 1)].rearrange("s p x -> p s x")
             nc.sync.dma_start(out=a_codes[g][:].bitcast(I32), in_=src.bitcast(I32))
 
         def load_a_scales():
-            nc.vector.memset(a_plane[:].rearrange("p s n -> p (s n)").bitcast(I32), 0)
-            for q in range(4):
-                src = a_scales[:, 4 * q : 4 * q + 4, :].rearrange("s r n -> r s n")
-                nc.sync.dma_start(out=a_plane[32 * q : 32 * q + 4, :, :].bitcast(I32), in_=src.bitcast(I32))
+            nc.vector.memset(a_scale_sb[:].rearrange("p s n -> p (s n)").bitcast(I32), 0)
+            for quad in range(4):
+                src = a_scales[:, 4 * quad : 4 * quad + 4, :].rearrange("s r n -> r s n")
+                nc.sync.dma_start(out=a_scale_sb[32 * quad : 32 * quad + 4, :, :].bitcast(I32), in_=src.bitcast(I32))
 
-        def load_b(g, h):
-            src = b[cols(g), cols(h)].rearrange("(p t) k -> p t k", t=4)
-            nc.sync.dma_start(out=b_raw[g][h][:], in_=src)
+        def load_b(x):
+            h, g = divmod(x, N_GROUPS)
+            nc.sync.dma_start(out=b_raw[g][h][:], in_=b[cols(g), cols(h)].rearrange("(p t) k -> p t k", t=PACK))
 
         def load_prior(i):
             nc.sync.dma_start(out=prior_sb[i][:], in_=prior[rows(i), :])
@@ -99,42 +103,37 @@ def tile_demand_estimation_gradient_s9_kernel(tc, d, a_words, a_scales, c, w, b,
                     at = (2 * s + u) * P
                     nc.tensor.transpose(bank[:, at : at + P], words[:, 256 * s + u : 256 * (s + 1) : 2], ident[:])
 
-        def pair_up(copy, dst, bank, groups):
-            width = groups * 2 * P
+        def pair_up(copy, dst, bank):
             copy(
-                out=dst.bitcast(F32).rearrange("p (g m u) -> p g m u", g=groups, u=2),
-                in_=bank[:, 0:width].rearrange("p (g u m) -> p g m u", g=groups, u=2),
+                out=dst.bitcast(F32).rearrange("p (s m u) -> p s m u", s=2, u=2),
+                in_=bank[:].rearrange("p (s u m) -> p s m u", s=2, u=2),
             )
 
-        def d_stage(i, count=1):
-            slot = i % 4
-            return d_t[:, slot * K : (slot + count) * K]
+        def d_slot(i, count=1):
+            return d_turned[:, (i % RING) * K : (i % RING + count) * K]
 
         def quantize_d(i, count=1):
-            span = slice(i * K // 4, (i + count) * K // 4)
-            nc.vector.quantize_mx(out=d_codes[:, span].bitcast(E4M3), scales=d_scales[:, span], in_=d_stage(i, count))
+            span = slice(i * K // PACK, (i + count) * K // PACK)
+            nc.vector.quantize_mx(out=d_codes[:, span].bitcast(E4M3), scales=d_scales[:, span], in_=d_slot(i, count))
 
         def spread_w():
             words = w_rows[:].bitcast(F32)
+            dst = w_all[:].bitcast(F32).rearrange("p (g u a j) -> p u g a j", g=N_GROUPS, u=2, j=4)
             for u in range(2):
                 for j in range(4):
-                    col = 2 * j + u
-                    nc.tensor.transpose(
-                        t_bank[u][:, j * P : (j + 1) * P], words[:, col : col + 1].to_broadcast([P, P]), ident[:]
-                    )
-                dst = w_all[:].bitcast(F32).rearrange("p (g u a j) -> p u g a j", g=N_GROUPS, u=2, j=4)
-                nc.scalar.copy(
-                    out=dst[:, u], in_=t_bank[u][:].rearrange("p (j g a) -> p g a j", j=4, g=N_GROUPS)
-                )
+                    column = words[:, 2 * j + u : 2 * j + u + 1].to_broadcast([P, P])
+                    nc.tensor.transpose(t_bank[u][:, j * P : (j + 1) * P], column, ident[:])
+                nc.scalar.copy(out=dst[:, u], in_=t_bank[u][:].rearrange("p (j g a) -> p g a j", j=4, g=N_GROUPS))
 
         def first_product(i, g):
             for s in range(K_PASSES):
+                span = slice((K_PASSES * i + s) * P, (K_PASSES * i + s + 1) * P)
                 nc.tensor.matmul_mx(
                     out=v_bank[g][:],
-                    lhsT=d_codes[:, (2 * i + s) * P : (2 * i + s + 1) * P].bitcast(E4M3),
-                    lhsT_scale=d_scales[:, (2 * i + s) * P : (2 * i + s + 1) * P],
+                    lhsT=d_codes[:, span].bitcast(E4M3),
+                    lhsT_scale=d_scales[:, span],
                     rhs=a_codes[g][:, s, :].bitcast(E2M1),
-                    rhs_scale=a_plane[:, s, cols(g)],
+                    rhs_scale=a_scale_sb[:, s, cols(g)],
                     start=(s == 0),
                     stop=(s == K_PASSES - 1),
                 )
@@ -148,174 +147,184 @@ def tile_demand_estimation_gradient_s9_kernel(tc, d, a_words, a_scales, c, w, b,
                 op=ALU.subtract,
             )
 
-        def weigh(engine, i, c0, c1):
-            span = slice(c0, c1)
+        def weigh(engine, i, first, end):
+            span = slice(first, end)
             engine.tensor_tensor(out=resid[i % 2][:, span], in0=diff[i % 2][:, span], in1=w_all[:, span], op=ALU.mult)
 
-        def turn_r(i, g0, g1):
-            bank = t_bank[g0 // 2]
+        def turn_r(i):
             words = resid[i % 2][:].bitcast(F32)
-            at = (g0 % 2) * 2 * P
-            for x in range(2 * (g1 - g0)):
-                first = 2 * g0 * P + x * P
-                nc.tensor.transpose(bank[:, at + x * P : at + (x + 1) * P], words[:, first : first + P], ident[:])
-            pair_up(nc.scalar.copy, resid_t[i % 2][:, g0 * BANK : g1 * BANK], bank[:, at:BANK], g1 - g0)
+            for y in range(2):
+                for quarter in range(4):
+                    at = (4 * y + quarter) * P
+                    nc.tensor.transpose(t_bank[y][:, rows(quarter)], words[:, at : at + P], ident[:])
+                pair_up(nc.scalar.copy, resid_turned[i % 2][:, y * N // 2 : (y + 1) * N // 2], t_bank[y])
 
         def quantize_r(i, g0, g1):
             nc.vector.quantize_mx(
                 out=r_codes[i][:, g0 * P : g1 * P].bitcast(E5M2),
                 scales=r_scales[i][:, g0 * P : g1 * P],
-                in_=resid_t[i % 2][:, g0 * BANK : g1 * BANK],
+                in_=resid_turned[i % 2][:, g0 * PASS : g1 * PASS],
             )
 
-        b_order = [(g, h) for h in range(K_HALVES) for g in range(N_GROUPS)]
-
-        def b_stage(x, count=1):
-            slot = (x + B_SHIFT) % 4
-            return b_grp[:, slot * 4 * BANK : (slot + count) * 4 * BANK]
+        def b_slot(x, count=1):
+            return b_grouped[:, (x % RING) * PACK * BANK : (x % RING + count) * PACK * BANK]
 
         def group_b(x, copy):
-            g, h = b_order[x]
+            h, g = divmod(x, N_GROUPS)
             copy(
-                out=b_stage(x).rearrange("p (a i t) -> p a t i", i=4, t=4),
+                out=b_slot(x).rearrange("p (a i t) -> p a t i", i=4, t=PACK),
                 in_=b_raw[g][h][:].rearrange("p t (a i) -> p a t i", i=4),
             )
 
-        def quantize_b(x, count=1):
+        def quantize_b(x, count):
             span = slice(x * BANK, (x + count) * BANK)
-            nc.vector.quantize_mx(out=b_codes[:, span].bitcast(E4M3), scales=b_scales[:, span], in_=b_stage(x, count))
+            nc.vector.quantize_mx(out=b_codes[:, span].bitcast(E4M3), scales=b_scales[:, span], in_=b_slot(x, count))
 
-        def second_product(i, h, bank, g0, g1):
-            for g in range(g0, g1):
+        def second_product(i, h, bank):
+            for g in range(N_GROUPS):
                 nc.tensor.matmul_mx(
                     out=bank[:],
-                    lhsT=r_codes[i][:, g * P : (g + 1) * P].bitcast(E5M2),
-                    lhsT_scale=r_scales[i][:, g * P : (g + 1) * P],
+                    lhsT=r_codes[i][:, rows(g)].bitcast(E5M2),
+                    lhsT_scale=r_scales[i][:, rows(g)],
                     rhs=b_codes[:, cols(h * N_GROUPS + g)].bitcast(E4M3),
                     rhs_scale=b_scales[:, cols(h * N_GROUPS + g)],
                     start=(g == 0),
                     stop=(g == N_GROUPS - 1),
                 )
 
-        def finish(x, i, h, bank):
-            stage = result[x % OUT_BUFS]
-            nc.vector.tensor_tensor(out=stage[:], in0=bank[:], in1=prior_sb[i][:, cols(h)], op=ALU.add)
-            nc.sync.dma_start(out=out[rows(i), cols(h)], in_=stage[:])
+        waiting = [(i, h) for i in range(ROW_TILES) for h in range(K_HALVES)]
+        in_psum = []
+        issued = []
+
+        def multiply(count, tiles_ready, halves_ready, banks):
+            ready = [(i, h) for i, h in waiting if i < tiles_ready and h < halves_ready]
+            for i, h in ready[:count]:
+                bank = banks[len(issued) % len(banks)]
+                second_product(i, h, bank)
+                in_psum.append((len(issued), i, h, bank))
+                issued.append((i, h))
+                waiting.remove((i, h))
+
+        def finish(count):
+            for block in in_psum[:count]:
+                number, i, h, bank = block
+                stage = result[number % RESULT_BUFS]
+                nc.vector.tensor_tensor(out=stage[:], in0=bank[:], in1=prior_sb[i][:, cols(h)], op=ALU.add)
+                nc.sync.dma_start(out=out[rows(i), cols(h)], in_=stage[:])
+                in_psum.remove(block)
+
+        def b_pieces_of_step(i):
+            return range(max(1, 2 * i), min(2 * i + 2, B_PIECES))
 
         make_identity(nc, ident[:])
-        last = ROW_TILES - 1
         nc.sync.dma_start(out=w_rows[:], in_=w.rearrange("(p x) -> p x", p=P))
         load_d(0)
         load_a_scales()
         load_a(0)
         load_c(0, 0)
+        load_b(0)
         load_d(1)
         load_a(1)
         load_a(2)
         load_c(0, 1)
-        load_b(*b_order[0])
         load_a(3)
-        for i in range(last):
-            if i % 2 == 0 and i + 3 <= last:
-                load_d(i + 2)
-                load_d(i + 3)
-            for x in range(max(1, 2 * i), min(2 * i + 2, len(b_order))):
-                load_b(*b_order[x])
-            load_c(i + 1, 0)
-            load_c(i + 1, 1)
-            if i == 2:
-                load_prior(0)
-            if i >= 2:
-                load_prior(i - 1)
-        load_prior(last - 1)
-        load_prior(last)
+        load_d(2)
+        load_d(3)
+        load_b(1)
+        load_c(1, 0)
+        load_c(1, 1)
+        load_b(2)
+        load_d(4)
+        load_d(5)
+        load_b(3)
+        load_c(2, 0)
+        load_c(2, 1)
+        load_b(4)
+        load_b(5)
+        load_d(6)
+        load_d(7)
+        load_c(3, 0)
+        load_c(3, 1)
+        load_prior(0)
+        load_prior(1)
+        load_b(6)
+        load_b(7)
+        for i in range(4, ROW_TILES):
+            load_c(i, 0)
+            load_c(i, 1)
+            load_prior(i - 2)
+        load_prior(LAST - 1)
+        load_prior(LAST)
 
         turn_d(0, o_bank[0])
-        pair_up(nc.vector.tensor_copy, d_stage(0), o_bank[0], K_PASSES)
+        pair_up(nc.vector.tensor_copy, d_slot(0), o_bank[0])
         quantize_d(0)
         spread_w()
+        group_b(0, nc.vector.tensor_copy)
         first_product(0, 0)
         turn_d(1, o_bank[1])
-        pair_up(nc.scalar.copy, d_stage(1), o_bank[1], K_PASSES)
+        pair_up(nc.scalar.copy, d_slot(1), o_bank[1])
         for g in range(1, N_GROUPS):
             first_product(0, g)
 
-        todo = [(i, h) for i in range(ROW_TILES) for h in range(K_HALVES)]
-        pending = []
-        issued = []
-
-        def multiply(count, tiles_ready, halves_ready, banks):
-            ready = [(i, h) for i, h in todo if i < tiles_ready and h < halves_ready]
-            for i, h in ready[:count]:
-                bank = banks[len(issued) % len(banks)]
-                second_product(i, h, bank, 0, N_GROUPS)
-                pending.append((len(issued), i, h, bank))
-                issued.append((i, h))
-                todo.remove((i, h))
-
-        def drain(count):
-            for block in pending[:count]:
-                finish(*block)
-                pending.remove(block)
-
-        def turn_d_pair(t, banks):
-            for y in range(2):
-                turn_d(t + y, banks[y])
-                pair_up(nc.scalar.copy, d_stage(t + y), banks[y], K_PASSES)
-
         for i in range(ROW_TILES):
-            halves_before = max(0, (i - 1) // 2)
-            halves_after = i // 2
-            turning = i % 2 == 0 and i + 3 <= last
-            if len(pending) == 2 and halves_before >= K_HALVES:
-                drain(1)
+            halves_ready = min(K_HALVES, max(0, i - 1) // 2)
+            if halves_ready == K_HALVES:
+                finish(1)
+            if i > 0:
+                turn_r(i - 1)
             if i == 0:
-                group_b(0, nc.scalar.copy)
-            else:
-                turn_r(i - 1, 0, 2)
-                turn_r(i - 1, 2, 4)
-            turn_late = len(pending) > 0
-            if turning and not turn_late:
-                turn_d_pair(i + 2, o_bank)
-            finishing = len(pending)
-            if halves_before >= K_HALVES:
-                multiply(1, i - 1, halves_before, o_bank)
-            finishing = len(pending)
-            for x in range(max(1, 2 * i), min(2 * i + 2, len(b_order))):
+                for y in range(2):
+                    turn_d(2 + y, o_bank[y])
+                    pair_up(nc.scalar.copy, d_slot(2 + y), o_bank[y])
+            if i == 2:
+                for y in range(2):
+                    pair_up(nc.scalar.copy, d_slot(4 + y), o_bank[y])
+            if i == 4:
+                pair_up(nc.scalar.copy, d_slot(6), o_bank[1])
+            if halves_ready == K_HALVES:
+                multiply(1, i - 1, halves_ready, o_bank)
+            for x in b_pieces_of_step(i):
                 group_b(x, nc.scalar.copy)
-            share = BANK if i == last else BANK + finishing * BANK // 2
+
+            gpsimd_end = BANK if i == LAST else BANK + len(in_psum) * GPSIMD_COLUMNS_PER_BLOCK
             for g in range(N_GROUPS):
                 subtract(i, g)
                 if g == 0:
                     weigh(nc.gpsimd, i, 0, BANK)
-                if g == 1 and share > BANK:
-                    weigh(nc.gpsimd, i, BANK, share)
-            if i == last:
+                if g == 1 and gpsimd_end > BANK:
+                    weigh(nc.gpsimd, i, BANK, gpsimd_end)
+            if i == LAST:
                 break
             if i == 0:
                 quantize_d(1)
             for g in range(N_GROUPS):
                 first_product(i + 1, g)
-            if turning and turn_late:
-                turn_d_pair(i + 2, [o_bank[len(issued) % 2], t_bank[0]])
-            drain(2)
-            if 0 < i <= N_GROUPS:
+            if i == 1:
+                for y in range(2):
+                    turn_d(4 + y, o_bank[y])
+            if i == 4:
+                turn_d(7, t_bank[0])
+                pair_up(nc.scalar.copy, d_slot(7), t_bank[0])
+            finish(2)
+            if i == 3:
+                turn_d(6, o_bank[1])
+            if 0 < i <= B_PIECES // 2:
                 quantize_b(2 * i - 2, 2)
             if i > 0:
                 quantize_r(i - 1, 0, N_GROUPS)
-            weigh(nc.vector, i, share, N)
-            if turning:
+            weigh(nc.vector, i, gpsimd_end, N)
+            if i in (0, 2, 4):
                 quantize_d(i + 2, 2)
-            multiply(2, i, halves_after, o_bank)
+            multiply(2, i, min(K_HALVES, i // 2), o_bank)
 
-        quantize_r(last - 1, 0, N_GROUPS)
-        weigh(nc.vector, last, BANK, N)
-        multiply(1, last, K_HALVES, v_bank)
-        turn_r(last, 0, 2)
-        turn_r(last, 2, 4)
-        drain(2)
-        multiply(1, last, K_HALVES, v_bank)
-        quantize_r(last, 0, 2)
-        quantize_r(last, 2, 4)
+        quantize_r(LAST - 1, 0, N_GROUPS)
+        weigh(nc.vector, LAST, BANK, N)
+        multiply(1, LAST, K_HALVES, v_bank)
+        turn_r(LAST)
+        finish(2)
+        multiply(1, LAST, K_HALVES, v_bank)
+        quantize_r(LAST, 0, N_GROUPS // 2)
+        quantize_r(LAST, N_GROUPS // 2, N_GROUPS)
         multiply(2, ROW_TILES, K_HALVES, v_bank)
-        drain(4)
+        finish(4)

from contextlib import ExitStack

import concourse.mybir as mybir
from concourse.masks import make_identity

M, K, N = 1024, 1024, 2048
FLOPS = 2 * 2 * M * K * N

F32 = mybir.dt.float32
BF16 = mybir.dt.bfloat16
I32 = mybir.dt.int32
U32 = mybir.dt.uint32
U8 = mybir.dt.uint8
E4M3 = mybir.dt.float8_e4m3fn_x4
E5M2 = mybir.dt.float8_e5m2_x4
E2M1 = mybir.dt.float4_e2m1fn_x4
ALU = mybir.AluOpType

P = 128
PACK = 4
PASS = P * PACK
BANK = 512
ROW_TILES = M // P
LAST = ROW_TILES - 1
K_PASSES = K // PASS
N_GROUPS = N // PASS
K_HALVES = K // BANK
B_PIECES = K_HALVES * N_GROUPS
RING = 4
RESULT_BUFS = 6
GPSIMD_COLUMNS_PER_BLOCK = BANK // 2


def tile_demand_estimation_gradient_s9_kernel(tc, d, a_words, a_scales, c, w, b, prior, out):
    nc = tc.nc
    with ExitStack() as ctx:
        sb = ctx.enter_context(tc.tile_pool(name="sb", bufs=1))
        ps = ctx.enter_context(tc.psum_pool(name="ps", bufs=1))
        ctx.enter_context(tc.manual_schedule())

        def sbuf(name, shape, dtype):
            return sb.tile(shape, dtype, name=name, align_bytes=64)

        ident = sbuf("ident", [P, P], F32)
        d_raw = [sbuf("d_raw%d" % i, [P, K], BF16) for i in range(ROW_TILES)]
        d_turned = sbuf("d_turned", [P, RING * K], BF16)
        d_codes = sbuf("d_codes", [P, ROW_TILES * K // PACK], U32)
        d_scales = sbuf("d_scales", [P, ROW_TILES * K // PACK], U8)
        a_codes = [sbuf("a_codes%d" % g, [P, K_PASSES, 2 * BANK], U8) for g in range(N_GROUPS)]
        a_scale_sb = sbuf("a_scale_sb", [P, K_PASSES, N], U8)
        c_raw = [[sbuf("c_raw%d_%d" % (i, y), [P, N // 2], BF16) for y in range(2)] for i in range(ROW_TILES)]
        w_rows = sbuf("w_rows", [P, N // P], BF16)
        w_all = sbuf("w_all", [P, N], BF16)
        b_raw = [[sbuf("b_raw%d_%d" % (g, h), [P, PACK, BANK], BF16) for h in range(K_HALVES)] for g in range(N_GROUPS)]
        b_grouped = sbuf("b_grouped", [P, RING * PACK * BANK], BF16)
        b_codes = sbuf("b_codes", [P, B_PIECES * BANK], U32)
        b_scales = sbuf("b_scales", [P, B_PIECES * BANK], U8)
        prior_sb = [sbuf("prior%d" % i, [P, K], BF16) for i in range(ROW_TILES)]
        diff = [sbuf("diff%d" % y, [P, N], F32) for y in range(2)]
        resid = [sbuf("resid%d" % y, [P, N], BF16) for y in range(2)]
        resid_turned = [sbuf("resid_turned%d" % y, [P, N], BF16) for y in range(2)]
        r_codes = [sbuf("r_codes%d" % i, [P, N // PACK], U32) for i in range(ROW_TILES)]
        r_scales = [sbuf("r_scales%d" % i, [P, N // PACK], U8) for i in range(ROW_TILES)]
        result = [sbuf("result%d" % y, [P, BANK], F32) for y in range(RESULT_BUFS)]

        v_bank = [ps.tile([P, BANK], F32, name="v_bank%d" % g) for g in range(N_GROUPS)]
        o_bank = [ps.tile([P, BANK], F32, name="o_bank%d" % y) for y in range(2)]
        t_bank = [ps.tile([P, BANK], F32, name="t_bank%d" % y) for y in range(2)]

        def rows(i):
            return slice(i * P, (i + 1) * P)

        def cols(g):
            return slice(g * BANK, (g + 1) * BANK)

        def load_d(i):
            nc.sync.dma_start(out=d_raw[i][:], in_=d[rows(i), :])

        def load_c(i, y):
            nc.sync.dma_start(out=c_raw[i][y][:], in_=c[rows(i), y * (N // 2) : (y + 1) * (N // 2)])

        def load_a(g):
            src = a_words[:, :, 2 * BANK * g : 2 * BANK * (g + 1)].rearrange("s p x -> p s x")
            nc.sync.dma_start(out=a_codes[g][:].bitcast(I32), in_=src.bitcast(I32))

        def load_a_scales():
            nc.vector.memset(a_scale_sb[:].rearrange("p s n -> p (s n)").bitcast(I32), 0)
            for quad in range(4):
                src = a_scales[:, 4 * quad : 4 * quad + 4, :].rearrange("s r n -> r s n")
                nc.sync.dma_start(out=a_scale_sb[32 * quad : 32 * quad + 4, :, :].bitcast(I32), in_=src.bitcast(I32))

        def load_b(x):
            h, g = divmod(x, N_GROUPS)
            nc.sync.dma_start(out=b_raw[g][h][:], in_=b[cols(g), cols(h)].rearrange("(p t) k -> p t k", t=PACK))

        def load_prior(i):
            nc.sync.dma_start(out=prior_sb[i][:], in_=prior[rows(i), :])

        def turn_d(i, bank):
            words = d_raw[i][:].bitcast(F32)
            for s in range(K_PASSES):
                for u in range(2):
                    at = (2 * s + u) * P
                    nc.tensor.transpose(bank[:, at : at + P], words[:, 256 * s + u : 256 * (s + 1) : 2], ident[:])

        def pair_up(copy, dst, bank):
            copy(
                out=dst.bitcast(F32).rearrange("p (s m u) -> p s m u", s=2, u=2),
                in_=bank[:].rearrange("p (s u m) -> p s m u", s=2, u=2),
            )

        def d_slot(i, count=1):
            return d_turned[:, (i % RING) * K : (i % RING + count) * K]

        def quantize_d(i, count=1):
            span = slice(i * K // PACK, (i + count) * K // PACK)
            nc.vector.quantize_mx(out=d_codes[:, span].bitcast(E4M3), scales=d_scales[:, span], in_=d_slot(i, count))

        def spread_w():
            words = w_rows[:].bitcast(F32)
            dst = w_all[:].bitcast(F32).rearrange("p (g u a j) -> p u g a j", g=N_GROUPS, u=2, j=4)
            for u in range(2):
                for j in range(4):
                    column = words[:, 2 * j + u : 2 * j + u + 1].to_broadcast([P, P])
                    nc.tensor.transpose(t_bank[u][:, j * P : (j + 1) * P], column, ident[:])
                nc.scalar.copy(out=dst[:, u], in_=t_bank[u][:].rearrange("p (j g a) -> p g a j", j=4, g=N_GROUPS))

        def first_product(i, g):
            for s in range(K_PASSES):
                span = slice((K_PASSES * i + s) * P, (K_PASSES * i + s + 1) * P)
                nc.tensor.matmul_mx(
                    out=v_bank[g][:],
                    lhsT=d_codes[:, span].bitcast(E4M3),
                    lhsT_scale=d_scales[:, span],
                    rhs=a_codes[g][:, s, :].bitcast(E2M1),
                    rhs_scale=a_scale_sb[:, s, cols(g)],
                    start=(s == 0),
                    stop=(s == K_PASSES - 1),
                )

        def subtract(i, g):
            natural = "p (j u e) -> p j u e"
            nc.vector.tensor_tensor(
                out=diff[i % 2][:, cols(g)].rearrange("p (u j e) -> p j u e", u=2, e=2),
                in0=v_bank[g][:].rearrange(natural, u=2, e=2),
                in1=c_raw[i][g // 2][:, cols(g % 2)].rearrange(natural, u=2, e=2),
                op=ALU.subtract,
            )

        def weigh(engine, i, first, end):
            span = slice(first, end)
            engine.tensor_tensor(out=resid[i % 2][:, span], in0=diff[i % 2][:, span], in1=w_all[:, span], op=ALU.mult)

        def turn_r(i):
            words = resid[i % 2][:].bitcast(F32)
            for y in range(2):
                for quarter in range(4):
                    at = (4 * y + quarter) * P
                    nc.tensor.transpose(t_bank[y][:, rows(quarter)], words[:, at : at + P], ident[:])
                pair_up(nc.scalar.copy, resid_turned[i % 2][:, y * N // 2 : (y + 1) * N // 2], t_bank[y])

        def quantize_r(i, g0, g1):
            nc.vector.quantize_mx(
                out=r_codes[i][:, g0 * P : g1 * P].bitcast(E5M2),
                scales=r_scales[i][:, g0 * P : g1 * P],
                in_=resid_turned[i % 2][:, g0 * PASS : g1 * PASS],
            )

        def b_slot(x, count=1):
            return b_grouped[:, (x % RING) * PACK * BANK : (x % RING + count) * PACK * BANK]

        def group_b(x, copy):
            h, g = divmod(x, N_GROUPS)
            copy(
                out=b_slot(x).rearrange("p (a i t) -> p a t i", i=4, t=PACK),
                in_=b_raw[g][h][:].rearrange("p t (a i) -> p a t i", i=4),
            )

        def quantize_b(x, count):
            span = slice(x * BANK, (x + count) * BANK)
            nc.vector.quantize_mx(out=b_codes[:, span].bitcast(E4M3), scales=b_scales[:, span], in_=b_slot(x, count))

        def second_product(i, h, bank):
            for g in range(N_GROUPS):
                nc.tensor.matmul_mx(
                    out=bank[:],
                    lhsT=r_codes[i][:, rows(g)].bitcast(E5M2),
                    lhsT_scale=r_scales[i][:, rows(g)],
                    rhs=b_codes[:, cols(h * N_GROUPS + g)].bitcast(E4M3),
                    rhs_scale=b_scales[:, cols(h * N_GROUPS + g)],
                    start=(g == 0),
                    stop=(g == N_GROUPS - 1),
                )

        waiting = [(i, h) for i in range(ROW_TILES) for h in range(K_HALVES)]
        in_psum = []
        issued = []

        def multiply(count, tiles_ready, halves_ready, banks):
            ready = [(i, h) for i, h in waiting if i < tiles_ready and h < halves_ready]
            for i, h in ready[:count]:
                bank = banks[len(issued) % len(banks)]
                second_product(i, h, bank)
                in_psum.append((len(issued), i, h, bank))
                issued.append((i, h))
                waiting.remove((i, h))

        def finish(count):
            for block in in_psum[:count]:
                number, i, h, bank = block
                stage = result[number % RESULT_BUFS]
                nc.vector.tensor_tensor(out=stage[:], in0=bank[:], in1=prior_sb[i][:, cols(h)], op=ALU.add)
                nc.sync.dma_start(out=out[rows(i), cols(h)], in_=stage[:])
                in_psum.remove(block)

        def b_pieces_of_step(i):
            return range(max(1, 2 * i), min(2 * i + 2, B_PIECES))

        make_identity(nc, ident[:])
        nc.sync.dma_start(out=w_rows[:], in_=w.rearrange("(p x) -> p x", p=P))
        load_d(0)
        load_a_scales()
        load_a(0)
        load_c(0, 0)
        load_b(0)
        load_d(1)
        load_a(1)
        load_a(2)
        load_c(0, 1)
        load_a(3)
        load_d(2)
        load_d(3)
        load_b(1)
        load_c(1, 0)
        load_c(1, 1)
        load_b(2)
        load_d(4)
        load_d(5)
        load_b(3)
        load_c(2, 0)
        load_c(2, 1)
        load_b(4)
        load_b(5)
        load_d(6)
        load_d(7)
        load_c(3, 0)
        load_c(3, 1)
        load_prior(0)
        load_prior(1)
        load_b(6)
        load_b(7)
        for i in range(4, ROW_TILES):
            load_c(i, 0)
            load_c(i, 1)
            load_prior(i - 2)
        load_prior(LAST - 1)
        load_prior(LAST)

        turn_d(0, o_bank[0])
        pair_up(nc.vector.tensor_copy, d_slot(0), o_bank[0])
        quantize_d(0)
        spread_w()
        group_b(0, nc.vector.tensor_copy)
        first_product(0, 0)
        turn_d(1, o_bank[1])
        pair_up(nc.scalar.copy, d_slot(1), o_bank[1])
        for g in range(1, N_GROUPS):
            first_product(0, g)

        for i in range(ROW_TILES):
            halves_ready = min(K_HALVES, max(0, i - 1) // 2)
            if halves_ready == K_HALVES:
                finish(1)
            if i > 0:
                turn_r(i - 1)
            if i == 0:
                for y in range(2):
                    turn_d(2 + y, o_bank[y])
                    pair_up(nc.scalar.copy, d_slot(2 + y), o_bank[y])
            if i == 2:
                for y in range(2):
                    pair_up(nc.scalar.copy, d_slot(4 + y), o_bank[y])
            if i == 4:
                pair_up(nc.scalar.copy, d_slot(6), o_bank[1])
            if halves_ready == K_HALVES:
                multiply(1, i - 1, halves_ready, o_bank)
            for x in b_pieces_of_step(i):
                group_b(x, nc.scalar.copy)

            gpsimd_end = BANK if i == LAST else BANK + len(in_psum) * GPSIMD_COLUMNS_PER_BLOCK
            for g in range(N_GROUPS):
                subtract(i, g)
                if g == 0:
                    weigh(nc.gpsimd, i, 0, BANK)
                if g == 1 and gpsimd_end > BANK:
                    weigh(nc.gpsimd, i, BANK, gpsimd_end)
            if i == LAST:
                break
            if i == 0:
                quantize_d(1)
            for g in range(N_GROUPS):
                first_product(i + 1, g)
            if i == 1:
                for y in range(2):
                    turn_d(4 + y, o_bank[y])
            if i == 4:
                turn_d(7, t_bank[0])
                pair_up(nc.scalar.copy, d_slot(7), t_bank[0])
            finish(2)
            if i == 3:
                turn_d(6, o_bank[1])
            if 0 < i <= B_PIECES // 2:
                quantize_b(2 * i - 2, 2)
            if i > 0:
                quantize_r(i - 1, 0, N_GROUPS)
            weigh(nc.vector, i, gpsimd_end, N)
            if i in (0, 2, 4):
                quantize_d(i + 2, 2)
            multiply(2, i, min(K_HALVES, i // 2), o_bank)

        quantize_r(LAST - 1, 0, N_GROUPS)
        weigh(nc.vector, LAST, BANK, N)
        multiply(1, LAST, K_HALVES, v_bank)
        turn_r(LAST)
        finish(2)
        multiply(1, LAST, K_HALVES, v_bank)
        quantize_r(LAST, 0, N_GROUPS // 2)
        quantize_r(LAST, N_GROUPS // 2, N_GROUPS)
        multiply(2, ROW_TILES, K_HALVES, v_bank)
        finish(4)
